import numpy as np
import ml_dtypes


def mxq(x, axis, fmt="e4m3"):
    dtype, down = {"e4m3": (ml_dtypes.float8_e4m3fn, 7), "e5m2": (ml_dtypes.float8_e5m2, 14)}[fmt]
    v = np.moveaxis(np.asarray(x, np.float32).astype(ml_dtypes.bfloat16).astype(np.float64), axis, -1)
    blocks = v.reshape(v.shape[:-1] + (-1, 32))
    amax = np.abs(blocks).max(-1, keepdims=True)
    byte = np.maximum(np.where(amax > 0, np.frexp(amax)[1] - 1 + 127, 0) - down, 1)
    scale = np.exp2(byte - 127.0)
    codes = (blocks / scale).astype(np.float32).astype(dtype).astype(np.float64)
    return np.moveaxis((codes * scale).reshape(v.shape), -1, axis)


WIDE = False


def mx_kscale(k):
    if not WIDE:
        return np.ones(k)
    levels = np.array([10, -10, 5, -5, 0])
    if k % 512:
        return np.exp2(np.random.permutation(np.resize(levels, k // 32))).repeat(32)
    a = np.empty((k // 512, 16))
    for p in range(k // 512):
        a[p, :8] = np.random.permutation(np.resize(levels, 8))
        for g in range(8):
            far = levels[np.abs(levels - a[p, g]) >= 10]
            a[p, g + 8] = far[np.random.randint(len(far))]
    return np.exp2(a.ravel()).repeat(32)


def f64(x):
    return np.asarray(x).astype(np.float64)


def striped(idx):
    return np.tile(idx.reshape(-1, 16).T, (8, 1)).astype(np.uint16)


def unstriped(offs):
    return offs[:16].T.reshape(-1).astype(np.int64)


def striped8(idx):
    return np.concatenate([x.reshape(-1, 16).T for x in idx]).astype(np.uint16)


def runs(offs, k):
    lists = np.stack([offs[16 * r : 16 * r + 16].T.reshape(-1) for r in range(8)]).astype(np.int64)
    return lists[np.arange(k) % 512 // 64]


def pack_weight(w):
    k, n = w.shape
    w = f64(np.asarray(w, np.float32).astype(ml_dtypes.bfloat16)).reshape(k // 32, 32, n)
    amax = np.abs(w).max(1)
    byte = np.clip(np.where(amax > 0, np.frexp(amax)[1] - 1 + 127 - 7, 1), 1, 254)
    scaled = (w * np.exp2(127.0 - byte)[:, None, :]).reshape(k, n).astype(np.float32)
    words = np.ascontiguousarray(scaled.reshape(k // 512, 128, 4, n).transpose(0, 1, 3, 2)).astype(ml_dtypes.float8_e4m3fn).view(np.uint8)
    return words, np.ascontiguousarray(byte.astype(np.uint8).reshape(k // 512, 16, n))


def unpack_weight(words, scales):
    g, p, n, _ = words.shape
    vals = np.ascontiguousarray(words).view(ml_dtypes.float8_e4m3fn).astype(np.float64) * np.repeat(np.exp2(scales.astype(np.float64) - 127.0), 8, axis=1)[..., None]
    return vals.transpose(0, 1, 3, 2).reshape(g * 512, n)


K, T, S, N, H, U = 512, 2048, 512, 512, 512, 1024


def setup_inputs():
    n = np.random.standard_normal
    s = mx_kscale(K)[:, None]
    u = mx_kscale(H)
    packed_xT = pack_weight(n((K, T)) * s)
    return {
        "x_words": packed_xT[0],
        "x_scales": packed_xT[1],
        "w1": (n((K, H)) / np.sqrt(K) / s).astype(np.float32),
        "w2": (n((K, H)) / np.sqrt(K) / s).astype(np.float32),
        "gn": (np.random.uniform(0.5, 1.5, (H, 1)) * u[:, None]).astype(np.float32),
        "w3": (n((H, N)) / np.sqrt(H) / u[:, None]).astype(np.float32),
        "mem": n((N, U)).astype(np.float32),
        "offs": striped(np.random.permutation(T)[:S]),
        "two": striped(np.random.permutation(T)[:S]),
        "n1": striped8(np.stack([np.random.permutation(S) for _ in range(8)])),
        "n2": striped8(np.stack([np.random.permutation(S) for _ in range(8)])),
        "n3": striped8(np.stack([np.random.permutation(U)[:S] for _ in range(8)])),
    }


def reference(x_words, x_scales, w1, w2, gn, w3, mem, offs, two, n1, n2, n3):
    xq = unpack_weight(x_words, x_scales)[:, unstriped(offs)]
    y = mxq(f64(w1), 0, "e4m3").T @ xq
    x_two = unpack_weight(x_words, x_scales)[:, unstriped(two)]
    d = mxq(f64(w2), 0, "e4m3").T @ x_two
    z = f64(gn) * (np.maximum(y, d[np.arange(H)[:, None], runs(n2, H)]) - (np.minimum(y[np.arange(H)[:, None], runs(n1, H)], d)))
    h = mxq(f64(w3), 0, "e4m3").T @ mxq(z, 0, "e4m3")
    out = f64(mem).copy()
    out[np.arange(N)[:, None], runs(n3, N)] = h
    return out

@@ -1,0 +1,200 @@
+from contextlib import ExitStack
+
+import concourse.mybir as mybir
+
+K, T, S, N, H, U = 512, 2048, 512, 512, 512, 1024
+FLOPS = 2 * S * (2 * K * H + H * N)
+
+F32 = mybir.dt.float32
+BF16 = mybir.dt.bfloat16
+I32 = mybir.dt.int32
+U32 = mybir.dt.uint32
+U16 = mybir.dt.uint16
+U8 = mybir.dt.uint8
+FP8X4 = mybir.dt.float8_e4m3fn_x4
+ALU = mybir.AluOpType
+COPY = mybir.ActivationFunctionType.Copy
+
+P = 128
+PACK = 4
+LIST_ROWS = 16
+CHUNK = 128
+CHUNKS = S // CHUNK
+BANK = 512
+
+
+def tile_picked_twlmaxbpage_none_p_kernel(
+    tc, x_words, x_scales, w1, w2, gn, w3, mem, offs, two, n1, n2, n3, out
+):
+    nc = tc.nc
+    with ExitStack() as ctx:
+        lists = ctx.enter_context(tc.tile_pool(name="lists", bufs=1))
+        keep = ctx.enter_context(tc.tile_pool(name="keep", bufs=1))
+        psum = ctx.enter_context(tc.psum_pool(name="psum", bufs=1))
+
+        def load_list(name, dram):
+            tile = lists.tile([P, S // LIST_ROWS], U16, name=name)
+            nc.sync.dma_start(tile[:], dram)
+            return tile
+
+        def load_weight(name, dram, pieces):
+            width = dram.shape[1] // pieces
+            rows = dram.rearrange("(p j) c -> p j c", j=PACK)
+            tiles = []
+            for h in range(pieces):
+                raw = keep.tile([P, PACK, width], F32, name=f"{name}_raw{h}")
+                nc.sync.dma_start(raw[:], rows[:, :, h * width : (h + 1) * width])
+                tiles.append(raw)
+            return tiles
+
+        def round_weight(copy, grouped, raw, h):
+            per = raw.shape[2] // PACK
+            dst = grouped[:].rearrange("p (t m j) -> p m j t", t=PACK, j=PACK)
+            copy(dst[:, h * per : (h + 1) * per], raw[:].rearrange("p j (m t) -> p m j t", t=PACK))
+
+        def quantize(name, grouped, width):
+            codes = keep.tile([P, width], U32, name=f"{name}_codes", align_bytes=64)
+            scales = keep.tile([P, width], U8, name=f"{name}_scales", align_bytes=64)
+            nc.vector.quantize_mx(out=codes[:].bitcast(FP8X4), scales=scales[:], in_=grouped)
+            return codes, scales
+
+        def product(acc, weight, t, moving):
+            cols = slice(t * P, (t + 1) * P)
+            nc.tensor.matmul_mx(
+                out=acc,
+                lhsT=weight[0][:, cols].bitcast(FP8X4),
+                lhsT_scale=weight[1][:, cols],
+                rhs=moving[0][:].bitcast(FP8X4),
+                rhs_scale=moving[1][:],
+                start=True,
+                stop=True,
+            )
+
+        xs = keep.tile([P, T], U8, name="xs")
+        nc.vector.memset(xs[:].bitcast(I32), 0)
+        xw = keep.tile([P, T], I32, name="xw")
+        nc.sync.dma_start(xw[:], x_words[0].rearrange("p n t -> p (n t)").bitcast(I32))
+        for q in range(4):
+            nc.sync.dma_start(
+                xs[32 * q : 32 * q + 4, :].bitcast(I32), x_scales[0, 4 * q : 4 * q + 4, :].bitcast(I32)
+            )
+        l_offs = load_list("l_offs", offs)
+        w1_raw = load_weight("w1", w1, 2)
+        l_two = load_list("l_two", two)
+        w2_raw = load_weight("w2", w2, 2)
+        l_n1 = load_list("l_n1", n1)
+        l_n2 = load_list("l_n2", n2)
+        gain = keep.tile([P, PACK], F32, name="gain")
+        nc.sync.dma_start(gain[:], gn.rearrange("(p t) o -> p (t o)", t=PACK))
+        w3_raw = load_weight("w3", w3, 1)
+        l_n3 = load_list("l_n3", n3)
+        mem_rows = mem.rearrange("(p t) u -> t p u", t=PACK)
+        out_rows = out.rearrange("(p t) u -> t p u", t=PACK)
+        pages = []
+        for t in range(PACK):
+            page = keep.tile([P, U], F32, name=f"page{t}")
+            nc.sync.dma_start(page[:], mem_rows[t])
+            pages.append(page)
+
+        def pick(name, window, dtype, lst):
+            got = keep.tile([P, S], dtype, name=name, align_bytes=64)
+            nc.vector.tensor_copy(got[:], window.indirect(lst[:]))
+            return got
+
+        w1_bf = keep.tile([P, PACK * H], BF16, name="w1_bf", align_bytes=64)
+        w2_bf = keep.tile([P, PACK * H], BF16, name="w2_bf", align_bytes=64)
+        w3_bf = keep.tile([P, PACK * N], BF16, name="w3_bf", align_bytes=64)
+
+        xa = (pick("xa_words", xw[:].bitcast(U32), U32, l_offs), pick("xa_scales", xs[:], U8, l_offs))
+        xb_words = pick("xb_words", xw[:].bitcast(U32), U32, l_two)
+        round_weight(nc.scalar.copy, w1_bf, w1_raw[0], 0)
+        round_weight(nc.scalar.copy, w1_bf, w1_raw[1], 1)
+        w1_q = quantize("w1", w1_bf[:], H)
+        xb = (xb_words, pick("xb_scales", xs[:], U8, l_two))
+        round_weight(nc.scalar.copy, w2_bf, w2_raw[0], 0)
+        round_weight(nc.vector.tensor_copy, w2_bf, w2_raw[1], 1)
+        w2_q = quantize("w2", w2_bf[:], H)
+
+        def project(name, weight, moving, first_bank):
+            banks, rows = [], []
+            for t in range(PACK):
+                acc = psum.tile([P, BANK], F32, name=f"bank{first_bank + t}")
+                product(acc[:], weight, t, moving)
+                row = keep.tile([P, S], F32, name=f"{name}{t}")
+                nc.scalar.copy(row[:], acc[:])
+                banks.append(acc)
+                rows.append(row)
+            return banks, rows
+
+        y_banks, y_rows = project("y", w1_q, xa, 0)
+        d_banks, d_rows = project("d", w2_q, xb, PACK)
+
+        def part(lst, c):
+            return lst[:, c * CHUNK // LIST_ROWS : (c + 1) * CHUNK // LIST_ROWS]
+
+        def cols(c):
+            return slice(c * CHUNK, (c + 1) * CHUNK)
+
+        gain_wide = gain[:].unsqueeze(1).to_broadcast([P, CHUNK, PACK])
+
+        def fetch(c):
+            got = keep.tile([P, 2, PACK, CHUNK], F32, name="got")
+            for i, (rows, lst) in enumerate(((y_rows, l_n1), (d_rows, l_n2))):
+                for t in range(PACK):
+                    nc.scalar.activation(got[:, i, t, :], rows[t][:].indirect(part(lst, c)), COPY)
+            return got
+
+        def layer(c, z_q):
+            h = keep.tile([P, PACK, CHUNK], F32, name=f"h{c}")
+            acc = psum.tile([P, PACK, CHUNK], F32, name=f"bank{c}")
+            for t in range(PACK):
+                product(acc[:, t, :], w3_q, t, z_q)
+            nc.scalar.copy(h[:], acc[:])
+            return h
+
+        def put(c, h, tiles):
+            for t in tiles:
+                nc.vector.tensor_copy(pages[t][:].indirect(part(l_n3, c)), h[:, t, :])
+                if c == CHUNKS - 1:
+                    nc.sync.dma_start(out_rows[t], pages[t][:])
+
+        def quantize_z(c, z_bf):
+            return quantize(f"z{c}", z_bf[:].rearrange("p j t -> p (j t)"), CHUNK)
+
+        first = keep.tile([P, 2, PACK, CHUNK], F32, name="first")
+        ends0 = keep.tile([P, 2, PACK, CHUNK], F32, name="ends0")
+        for t in range(PACK):
+            nc.vector.tensor_copy(first[:, 0, t, :], y_rows[t][:].indirect(part(l_n1, 0)))
+        round_weight(nc.vector.tensor_copy, w3_bf, w3_raw[0], 0)
+        w3_q = quantize("w3", w3_bf[:], N)
+        for t in range(PACK):
+            nc.vector.tensor_copy(first[:, 1, t, :], d_rows[t][:].indirect(part(l_n2, 0)))
+            nc.vector.tensor_tensor(ends0[:, 0, t, :], d_banks[t][:, cols(0)], first[:, 0, t, :], ALU.min)
+            nc.vector.tensor_tensor(ends0[:, 1, t, :], y_banks[t][:, cols(0)], first[:, 1, t, :], ALU.max)
+        gap0 = keep.tile([P, PACK, CHUNK], F32, name="gap0")
+        nc.vector.tensor_tensor(gap0[:], ends0[:, 1], ends0[:, 0], ALU.subtract)
+        z_bf = keep.tile([P, CHUNK, PACK], BF16, name="z_bf0", align_bytes=64)
+        nc.vector.tensor_tensor(z_bf[:], gap0[:].rearrange("p t j -> p j t"), gain_wide, ALU.mult)
+        got = fetch(1)
+        z_q = quantize_z(0, z_bf)
+        for c in range(1, CHUNKS):
+            h = layer(c - 1, z_q)
+            for t in range(PACK):
+                nc.vector.tensor_tensor(got[:, 0, t, :], got[:, 0, t, :], d_rows[t][:, cols(c)], ALU.min)
+            for t in range(PACK):
+                nc.vector.tensor_tensor(got[:, 1, t, :], y_rows[t][:, cols(c)], got[:, 1, t, :], ALU.max)
+            gap = keep.tile([P, PACK, CHUNK], F32, name=f"gap{c}")
+            nc.vector.tensor_tensor(gap[:], got[:, 1], got[:, 0], ALU.subtract)
+            planes = keep.tile([P, PACK, CHUNK], BF16, name=f"planes{c}")
+            for t in range(PACK):
+                nc.scalar.activation(planes[:, t, :], gap[:, t, :], COPY, scale=gain[:, t : t + 1])
+            z_bf = keep.tile([P, CHUNK, PACK], BF16, name=f"z_bf{c}", align_bytes=64)
+            nc.scalar.copy(
+                z_bf[:].rearrange("p (g i) t -> p g t i", i=PACK), planes[:].rearrange("p t (g i) -> p g t i", i=PACK)
+            )
+            if c + 1 < CHUNKS:
+                got = fetch(c + 1)
+            put(c - 1, h, range(2))
+            z_q = quantize_z(c, z_bf)
+            put(c - 1, h, range(2, PACK))
+        put(CHUNKS - 1, layer(CHUNKS - 1, z_q), range(PACK))

@@ -88,20 +88,20 @@ def tile_picked_twlmaxbpage_none_p_kernel(
         nc.sync.dma_start(gain[:], gn.rearrange("(p t) o -> p (t o)", t=PACK))
         w3_raw = load_weight("w3", w3, 1)
         l_n3 = load_list("l_n3", n3)
-        mem_rows = mem.rearrange("(p t) u -> t p u", t=PACK)
-        out_rows = out.rearrange("(p t) u -> t p u", t=PACK)
+        mem_rows = mem.rearrange("(b t r) u -> t b r u", t=PACK, r=8)
+        out_rows = out.rearrange("(b t r) u -> t b r u", t=PACK, r=8)
         pages = []
         for t in range(PACK):
             page = keep.tile([P, U], F32, name=f"page{t}")
             nc.sync.dma_start(page[:], mem_rows[t])
             pages.append(page)
 
-        def pick(name, window, dtype, lst):
-            got = keep.tile([P, S], dtype, name=name, align_bytes=64)
+        def pick(name, window, dtype, lst, tag=None):
+            got = keep.tile([P, S], dtype, name=name, tag=tag or name, align_bytes=64)
             nc.vector.tensor_copy(got[:], window.indirect(lst[:]))
             return got
 
-        w1_bf = keep.tile([P, PACK * H], BF16, name="w1_bf", align_bytes=64)
+        w1_bf = keep.tile([P, PACK * H], BF16, name="w1_bf", tag="w1_bf", align_bytes=64)
         w2_bf = keep.tile([P, PACK * H], BF16, name="w2_bf", align_bytes=64)
         w3_bf = keep.tile([P, PACK * N], BF16, name="w3_bf", align_bytes=64)
 
@@ -110,24 +110,30 @@ def tile_picked_twlmaxbpage_none_p_kernel(
         round_weight(nc.scalar.copy, w1_bf, w1_raw[0], 0)
         round_weight(nc.scalar.copy, w1_bf, w1_raw[1], 1)
         w1_q = quantize("w1", w1_bf[:], H)
-        xb = (xb_words, pick("xb_scales", xs[:], U8, l_two))
+        xb = (xb_words, pick("xb_scales", xs[:], U8, l_two, "w1_bf"))
         round_weight(nc.scalar.copy, w2_bf, w2_raw[0], 0)
         round_weight(nc.vector.tensor_copy, w2_bf, w2_raw[1], 1)
         w2_q = quantize("w2", w2_bf[:], H)
 
-        def project(name, weight, moving, first_bank):
-            banks, rows = [], []
+        def project(weight, moving, first_bank):
+            banks = []
             for t in range(PACK):
                 acc = psum.tile([P, BANK], F32, name=f"bank{first_bank + t}")
                 product(acc[:], weight, t, moving)
-                row = keep.tile([P, S], F32, name=f"{name}{t}")
-                nc.scalar.copy(row[:], acc[:])
                 banks.append(acc)
-                rows.append(row)
-            return banks, rows
+            return banks
 
-        y_banks, y_rows = project("y", w1_q, xa, 0)
-        d_banks, d_rows = project("d", w2_q, xb, PACK)
+        def copy_out(name, banks):
+            rows = []
+            for t in range(PACK):
+                row = keep.tile([P, S], F32, name=f"{name}{t}")
+                nc.scalar.copy(row[:], banks[t][:])
+                rows.append(row)
+            return rows
+
+        y_banks = project(w1_q, xa, 0)
+        y_rows = copy_out("y", y_banks)
+        d_banks = project(w2_q, xb, PACK)
 
         def part(lst, c):
             return lst[:, c * CHUNK // LIST_ROWS : (c + 1) * CHUNK // LIST_ROWS]
@@ -144,18 +150,18 @@ def tile_picked_twlmaxbpage_none_p_kernel(
                     nc.scalar.activation(got[:, i, t, :], rows[t][:].indirect(part(lst, c)), COPY)
             return got
 
-        def layer(c, z_q):
-            h = keep.tile([P, PACK, CHUNK], F32, name=f"h{c}")
-            acc = psum.tile([P, PACK, CHUNK], F32, name=f"bank{c}")
-            for t in range(PACK):
-                product(acc[:, t, :], w3_q, t, z_q)
+        def layer(c, z_q, tiles, bank):
+            h = keep.tile([P, len(tiles), CHUNK], F32, name=f"h{c}_{tiles[0]}")
+            acc = psum.tile([P, len(tiles), CHUNK], F32, name=f"bank{bank}")
+            for i, t in enumerate(tiles):
+                product(acc[:, i, :], w3_q, t, z_q)
             nc.scalar.copy(h[:], acc[:])
-            return h
+            return [(t, part(l_n3, c), h[:, i, :]) for i, t in enumerate(tiles)]
 
-        def put(c, h, tiles):
-            for t in tiles:
-                nc.vector.tensor_copy(pages[t][:].indirect(part(l_n3, c)), h[:, t, :])
-                if c == CHUNKS - 1:
+        def put(jobs, last):
+            for t, where, values in jobs:
+                nc.vector.tensor_copy(pages[t][:].indirect(where), values)
+                if last:
                     nc.sync.dma_start(out_rows[t], pages[t][:])
 
         def quantize_z(c, z_bf):
@@ -165,36 +171,52 @@ def tile_picked_twlmaxbpage_none_p_kernel(
         ends0 = keep.tile([P, 2, PACK, CHUNK], F32, name="ends0")
         for t in range(PACK):
             nc.vector.tensor_copy(first[:, 0, t, :], y_rows[t][:].indirect(part(l_n1, 0)))
-        round_weight(nc.vector.tensor_copy, w3_bf, w3_raw[0], 0)
-        w3_q = quantize("w3", w3_bf[:], N)
         for t in range(PACK):
-            nc.vector.tensor_copy(first[:, 1, t, :], d_rows[t][:].indirect(part(l_n2, 0)))
             nc.vector.tensor_tensor(ends0[:, 0, t, :], d_banks[t][:, cols(0)], first[:, 0, t, :], ALU.min)
-            nc.vector.tensor_tensor(ends0[:, 1, t, :], y_banks[t][:, cols(0)], first[:, 1, t, :], ALU.max)
+        d_rows = copy_out("d", d_banks)
+        w3_src = w3_raw[0][:].rearrange("p j (b t r) -> p t b r j", t=PACK, r=8)
+        w3_dst = w3_bf[:].rearrange("p (t b r j) -> p t b r j", t=PACK, r=8, j=PACK)
+        for t in range(PACK):
+            nc.gpsimd.tensor_scalar(w3_dst[:, t], w3_src[:, t], 1.0, 0.0, ALU.mult, ALU.add)
+        for t in range(PACK):
+            if t < 2:
+                nc.vector.tensor_copy(first[:, 1, t, :], d_rows[t][:].indirect(part(l_n2, 0)))
+            else:
+                nc.scalar.activation(first[:, 1, t, :], d_rows[t][:].indirect(part(l_n2, 0)), COPY)
+            if t > 0:
+                nc.vector.tensor_tensor(ends0[:, 1, t - 1, :], y_banks[t - 1][:, cols(0)], first[:, 1, t - 1, :], ALU.max)
+        nc.vector.tensor_tensor(ends0[:, 1, PACK - 1, :], y_banks[PACK - 1][:, cols(0)], first[:, 1, PACK - 1, :], ALU.max)
         gap0 = keep.tile([P, PACK, CHUNK], F32, name="gap0")
         nc.vector.tensor_tensor(gap0[:], ends0[:, 1], ends0[:, 0], ALU.subtract)
-        z_bf = keep.tile([P, CHUNK, PACK], BF16, name="z_bf0", align_bytes=64)
+        w3_q = quantize("w3", w3_bf[:], N)
+        z_bf = keep.tile([P, CHUNK, PACK], BF16, name="z_bf0", tag="ring", align_bytes=64)
         nc.vector.tensor_tensor(z_bf[:], gap0[:].rearrange("p t j -> p j t"), gain_wide, ALU.mult)
         got = fetch(1)
         z_q = quantize_z(0, z_bf)
+        late_acc = psum.tile([P, 2, CHUNK], F32, name="bank0")
         for c in range(1, CHUNKS):
-            h = layer(c - 1, z_q)
+            if c == 1:
+                jobs = layer(0, z_q, [0], 4) + layer(0, z_q, [1, 2, 3], 5)
+            elif c == 2:
+                jobs = layer(1, z_q, [0, 1, 2, 3], 6)
+            else:
+                jobs = layer(2, z_q, [0, 1, 2], 7)
+                product(late_acc[:, 0, :], w3_q, 3, z_q)
+            ends = keep.tile([P, 2, PACK, CHUNK], F32, name=f"ends{c}", tag="ring", align_bytes=64)
             for t in range(PACK):
-                nc.vector.tensor_tensor(got[:, 0, t, :], got[:, 0, t, :], d_rows[t][:, cols(c)], ALU.min)
+                nc.vector.tensor_tensor(ends[:, 0, t, :], got[:, 0, t, :], d_rows[t][:, cols(c)], ALU.min)
             for t in range(PACK):
-                nc.vector.tensor_tensor(got[:, 1, t, :], y_rows[t][:, cols(c)], got[:, 1, t, :], ALU.max)
-            gap = keep.tile([P, PACK, CHUNK], F32, name=f"gap{c}")
-            nc.vector.tensor_tensor(gap[:], got[:, 1], got[:, 0], ALU.subtract)
-            planes = keep.tile([P, PACK, CHUNK], BF16, name=f"planes{c}")
-            for t in range(PACK):
-                nc.scalar.activation(planes[:, t, :], gap[:, t, :], COPY, scale=gain[:, t : t + 1])
-            z_bf = keep.tile([P, CHUNK, PACK], BF16, name=f"z_bf{c}", align_bytes=64)
-            nc.scalar.copy(
-                z_bf[:].rearrange("p (g i) t -> p g t i", i=PACK), planes[:].rearrange("p t (g i) -> p g t i", i=PACK)
-            )
+                nc.vector.tensor_tensor(ends[:, 1, t, :], y_rows[t][:, cols(c)], got[:, 1, t, :], ALU.max)
             if c + 1 < CHUNKS:
                 got = fetch(c + 1)
-            put(c - 1, h, range(2))
+            gap = keep.tile([P, PACK, CHUNK], F32, name=f"gap{c}")
+            nc.gpsimd.tensor_tensor(gap[:], ends[:, 1], ends[:, 0], ALU.subtract)
+            z_bf = keep.tile([P, CHUNK, PACK], BF16, name=f"z_bf{c}", tag="ring", align_bytes=64)
+            nc.gpsimd.tensor_tensor(z_bf[:], gap[:].rearrange("p t j -> p j t"), gain_wide, ALU.mult)
+            put(jobs, False)
             z_q = quantize_z(c, z_bf)
-            put(c - 1, h, range(2, PACK))
-        put(CHUNKS - 1, layer(CHUNKS - 1, z_q), range(PACK))
+        jobs = layer(3, z_q, [0], 1) + layer(3, z_q, [1, 2], 2)
+        product(late_acc[:, 1, :], w3_q, 3, z_q)
+        late = keep.tile([P, 2 * CHUNK], F32, name="late")
+        nc.scalar.copy(late[:], late_acc[:].rearrange("p c j -> p (c j)"))
+        put(jobs + [(3, l_n3[:, 2 * CHUNK // LIST_ROWS :], late[:])], True)

@@ -88,8 +88,8 @@ def tile_picked_twlmaxbpage_none_p_kernel(
         nc.sync.dma_start(gain[:], gn.rearrange("(p t) o -> p (t o)", t=PACK))
         w3_raw = load_weight("w3", w3, 1)
         l_n3 = load_list("l_n3", n3)
-        mem_rows = mem.rearrange("(b t r) u -> t b r u", t=PACK, r=8)
-        out_rows = out.rearrange("(b t r) u -> t b r u", t=PACK, r=8)
+        mem_rows = mem.rearrange("(p t) u -> t p u", t=PACK)
+        out_rows = out.rearrange("(p t) u -> t p u", t=PACK)
         pages = []
         for t in range(PACK):
             page = keep.tile([P, U], F32, name=f"page{t}")
@@ -103,10 +103,9 @@ def tile_picked_twlmaxbpage_none_p_kernel(
 
         w1_bf = keep.tile([P, PACK * H], BF16, name="w1_bf", tag="w1_bf", align_bytes=64)
         w2_bf = keep.tile([P, PACK * H], BF16, name="w2_bf", align_bytes=64)
-        w3_bf = keep.tile([P, PACK * N], BF16, name="w3_bf", align_bytes=64)
 
         xa = (pick("xa_words", xw[:].bitcast(U32), U32, l_offs), pick("xa_scales", xs[:], U8, l_offs))
-        xb_words = pick("xb_words", xw[:].bitcast(U32), U32, l_two)
+        xb_words = pick("xb_words", xw[:].bitcast(U32), U32, l_two, "got")
         round_weight(nc.scalar.copy, w1_bf, w1_raw[0], 0)
         round_weight(nc.scalar.copy, w1_bf, w1_raw[1], 1)
         w1_q = quantize("w1", w1_bf[:], H)
@@ -115,25 +114,19 @@ def tile_picked_twlmaxbpage_none_p_kernel(
         round_weight(nc.vector.tensor_copy, w2_bf, w2_raw[1], 1)
         w2_q = quantize("w2", w2_bf[:], H)
 
-        def project(weight, moving, first_bank):
-            banks = []
+        def project(name, weight, moving, first_bank):
+            banks, rows = [], []
             for t in range(PACK):
                 acc = psum.tile([P, BANK], F32, name=f"bank{first_bank + t}")
                 product(acc[:], weight, t, moving)
-                banks.append(acc)
-            return banks
-
-        def copy_out(name, banks):
-            rows = []
-            for t in range(PACK):
                 row = keep.tile([P, S], F32, name=f"{name}{t}")
-                nc.scalar.copy(row[:], banks[t][:])
+                nc.scalar.copy(row[:], acc[:])
+                banks.append(acc)
                 rows.append(row)
-            return rows
+            return banks, rows
 
-        y_banks = project(w1_q, xa, 0)
-        y_rows = copy_out("y", y_banks)
-        d_banks = project(w2_q, xb, PACK)
+        y_banks, y_rows = project("y", w1_q, xa, 0)
+        d_banks, d_rows = project("d", w2_q, xb, PACK)
 
         def part(lst, c):
             return lst[:, c * CHUNK // LIST_ROWS : (c + 1) * CHUNK // LIST_ROWS]
@@ -144,7 +137,7 @@ def tile_picked_twlmaxbpage_none_p_kernel(
         gain_wide = gain[:].unsqueeze(1).to_broadcast([P, CHUNK, PACK])
 
         def fetch(c):
-            got = keep.tile([P, 2, PACK, CHUNK], F32, name="got")
+            got = keep.tile([P, 2, PACK, CHUNK], F32, name="got", align_bytes=64)
             for i, (rows, lst) in enumerate(((y_rows, l_n1), (d_rows, l_n2))):
                 for t in range(PACK):
                     nc.scalar.activation(got[:, i, t, :], rows[t][:].indirect(part(lst, c)), COPY)
@@ -167,30 +160,22 @@ def tile_picked_twlmaxbpage_none_p_kernel(
         def quantize_z(c, z_bf):
             return quantize(f"z{c}", z_bf[:].rearrange("p j t -> p (j t)"), CHUNK)
 
+        w3_bf = keep.tile([P, PACK * N], BF16, name="w3_bf", tag="w2_codes", align_bytes=64)
+        round_weight(nc.scalar.copy, w3_bf, w3_raw[0], 0)
+
         first = keep.tile([P, 2, PACK, CHUNK], F32, name="first")
         ends0 = keep.tile([P, 2, PACK, CHUNK], F32, name="ends0")
         for t in range(PACK):
             nc.vector.tensor_copy(first[:, 0, t, :], y_rows[t][:].indirect(part(l_n1, 0)))
         for t in range(PACK):
+            nc.vector.tensor_copy(first[:, 1, t, :], d_rows[t][:].indirect(part(l_n2, 0)))
             nc.vector.tensor_tensor(ends0[:, 0, t, :], d_banks[t][:, cols(0)], first[:, 0, t, :], ALU.min)
-        d_rows = copy_out("d", d_banks)
-        w3_src = w3_raw[0][:].rearrange("p j (b t r) -> p t b r j", t=PACK, r=8)
-        w3_dst = w3_bf[:].rearrange("p (t b r j) -> p t b r j", t=PACK, r=8, j=PACK)
-        for t in range(PACK):
-            nc.gpsimd.tensor_scalar(w3_dst[:, t], w3_src[:, t], 1.0, 0.0, ALU.mult, ALU.add)
-        for t in range(PACK):
-            if t < 2:
-                nc.vector.tensor_copy(first[:, 1, t, :], d_rows[t][:].indirect(part(l_n2, 0)))
-            else:
-                nc.scalar.activation(first[:, 1, t, :], d_rows[t][:].indirect(part(l_n2, 0)), COPY)
-            if t > 0:
-                nc.vector.tensor_tensor(ends0[:, 1, t - 1, :], y_banks[t - 1][:, cols(0)], first[:, 1, t - 1, :], ALU.max)
-        nc.vector.tensor_tensor(ends0[:, 1, PACK - 1, :], y_banks[PACK - 1][:, cols(0)], first[:, 1, PACK - 1, :], ALU.max)
+            nc.vector.tensor_tensor(ends0[:, 1, t, :], y_banks[t][:, cols(0)], first[:, 1, t, :], ALU.max)
         gap0 = keep.tile([P, PACK, CHUNK], F32, name="gap0")
         nc.vector.tensor_tensor(gap0[:], ends0[:, 1], ends0[:, 0], ALU.subtract)
-        w3_q = quantize("w3", w3_bf[:], N)
         z_bf = keep.tile([P, CHUNK, PACK], BF16, name="z_bf0", tag="ring", align_bytes=64)
         nc.vector.tensor_tensor(z_bf[:], gap0[:].rearrange("p t j -> p j t"), gain_wide, ALU.mult)
+        w3_q = quantize("w3", w3_bf[:], N)
         got = fetch(1)
         z_q = quantize_z(0, z_bf)
         late_acc = psum.tile([P, 2, CHUNK], F32, name="bank0")

from contextlib import ExitStack

import concourse.mybir as mybir

K, T, S, N, H, U = 512, 2048, 512, 512, 512, 1024
FLOPS = 2 * S * (2 * K * H + H * N)

F32 = mybir.dt.float32
BF16 = mybir.dt.bfloat16
I32 = mybir.dt.int32
U32 = mybir.dt.uint32
U16 = mybir.dt.uint16
U8 = mybir.dt.uint8
FP8X4 = mybir.dt.float8_e4m3fn_x4
ALU = mybir.AluOpType
COPY = mybir.ActivationFunctionType.Copy

P = 128
PACK = 4
LIST_ROWS = 16
CHUNK = 128
CHUNKS = S // CHUNK
BANK = 512


def tile_picked_twlmaxbpage_none_p_kernel(
    tc, x_words, x_scales, w1, w2, gn, w3, mem, offs, two, n1, n2, n3, out
):
    nc = tc.nc
    with ExitStack() as ctx:
        lists = ctx.enter_context(tc.tile_pool(name="lists", bufs=1))
        keep = ctx.enter_context(tc.tile_pool(name="keep", bufs=1))
        psum = ctx.enter_context(tc.psum_pool(name="psum", bufs=1))

        def load_list(name, dram):
            tile = lists.tile([P, S // LIST_ROWS], U16, name=name)
            nc.sync.dma_start(tile[:], dram)
            return tile

        def load_weight(name, dram, pieces):
            width = dram.shape[1] // pieces
            rows = dram.rearrange("(p j) c -> p j c", j=PACK)
            tiles = []
            for h in range(pieces):
                raw = keep.tile([P, PACK, width], F32, name=f"{name}_raw{h}")
                nc.sync.dma_start(raw[:], rows[:, :, h * width : (h + 1) * width])
                tiles.append(raw)
            return tiles

        def round_weight(copy, grouped, raw, h):
            per = raw.shape[2] // PACK
            dst = grouped[:].rearrange("p (t m j) -> p m j t", t=PACK, j=PACK)
            copy(dst[:, h * per : (h + 1) * per], raw[:].rearrange("p j (m t) -> p m j t", t=PACK))

        def quantize(name, grouped, width):
            codes = keep.tile([P, width], U32, name=f"{name}_codes", align_bytes=64)
            scales = keep.tile([P, width], U8, name=f"{name}_scales", align_bytes=64)
            nc.vector.quantize_mx(out=codes[:].bitcast(FP8X4), scales=scales[:], in_=grouped)
            return codes, scales

        def product(acc, weight, t, moving):
            cols = slice(t * P, (t + 1) * P)
            nc.tensor.matmul_mx(
                out=acc,
                lhsT=weight[0][:, cols].bitcast(FP8X4),
                lhsT_scale=weight[1][:, cols],
                rhs=moving[0][:].bitcast(FP8X4),
                rhs_scale=moving[1][:],
                start=True,
                stop=True,
            )

        xs = keep.tile([P, T], U8, name="xs")
        nc.vector.memset(xs[:].bitcast(I32), 0)
        xw = keep.tile([P, T], I32, name="xw")
        nc.sync.dma_start(xw[:], x_words[0].rearrange("p n t -> p (n t)").bitcast(I32))
        for q in range(4):
            nc.sync.dma_start(
                xs[32 * q : 32 * q + 4, :].bitcast(I32), x_scales[0, 4 * q : 4 * q + 4, :].bitcast(I32)
            )
        l_offs = load_list("l_offs", offs)
        w1_raw = load_weight("w1", w1, 2)
        l_two = load_list("l_two", two)
        w2_raw = load_weight("w2", w2, 2)
        l_n1 = load_list("l_n1", n1)
        l_n2 = load_list("l_n2", n2)
        gain = keep.tile([P, PACK], F32, name="gain")
        nc.sync.dma_start(gain[:], gn.rearrange("(p t) o -> p (t o)", t=PACK))
        w3_raw = load_weight("w3", w3, 1)
        l_n3 = load_list("l_n3", n3)
        mem_rows = mem.rearrange("(p t) u -> t p u", t=PACK)
        out_rows = out.rearrange("(p t) u -> t p u", t=PACK)
        pages = []
        for t in range(PACK):
            page = keep.tile([P, U], F32, name=f"page{t}")
            nc.sync.dma_start(page[:], mem_rows[t])
            pages.append(page)

        def pick(name, window, dtype, lst, tag=None):
            got = keep.tile([P, S], dtype, name=name, tag=tag or name, align_bytes=64)
            nc.vector.tensor_copy(got[:], window.indirect(lst[:]))
            return got

        w1_bf = keep.tile([P, PACK * H], BF16, name="w1_bf", tag="w1_bf", align_bytes=64)
        w2_bf = keep.tile([P, PACK * H], BF16, name="w2_bf", align_bytes=64)

        xa = (pick("xa_words", xw[:].bitcast(U32), U32, l_offs), pick("xa_scales", xs[:], U8, l_offs))
        xb_words = pick("xb_words", xw[:].bitcast(U32), U32, l_two, "got")
        round_weight(nc.scalar.copy, w1_bf, w1_raw[0], 0)
        round_weight(nc.scalar.copy, w1_bf, w1_raw[1], 1)
        w1_q = quantize("w1", w1_bf[:], H)
        xb = (xb_words, pick("xb_scales", xs[:], U8, l_two, "w1_bf"))
        round_weight(nc.scalar.copy, w2_bf, w2_raw[0], 0)
        round_weight(nc.vector.tensor_copy, w2_bf, w2_raw[1], 1)
        w2_q = quantize("w2", w2_bf[:], H)

        def project(name, weight, moving, first_bank):
            banks, rows = [], []
            for t in range(PACK):
                acc = psum.tile([P, BANK], F32, name=f"bank{first_bank + t}")
                product(acc[:], weight, t, moving)
                row = keep.tile([P, S], F32, name=f"{name}{t}")
                nc.scalar.copy(row[:], acc[:])
                banks.append(acc)
                rows.append(row)
            return banks, rows

        y_banks, y_rows = project("y", w1_q, xa, 0)
        d_banks, d_rows = project("d", w2_q, xb, PACK)

        def part(lst, c):
            return lst[:, c * CHUNK // LIST_ROWS : (c + 1) * CHUNK // LIST_ROWS]

        def cols(c):
            return slice(c * CHUNK, (c + 1) * CHUNK)

        gain_wide = gain[:].unsqueeze(1).to_broadcast([P, CHUNK, PACK])

        def fetch(c):
            got = keep.tile([P, 2, PACK, CHUNK], F32, name="got", align_bytes=64)
            for i, (rows, lst) in enumerate(((y_rows, l_n1), (d_rows, l_n2))):
                for t in range(PACK):
                    nc.scalar.activation(got[:, i, t, :], rows[t][:].indirect(part(lst, c)), COPY)
            return got

        def layer(c, z_q, tiles, bank):
            h = keep.tile([P, len(tiles), CHUNK], F32, name=f"h{c}_{tiles[0]}")
            acc = psum.tile([P, len(tiles), CHUNK], F32, name=f"bank{bank}")
            for i, t in enumerate(tiles):
                product(acc[:, i, :], w3_q, t, z_q)
            nc.scalar.copy(h[:], acc[:])
            return [(t, part(l_n3, c), h[:, i, :]) for i, t in enumerate(tiles)]

        def put(jobs, last):
            for t, where, values in jobs:
                nc.vector.tensor_copy(pages[t][:].indirect(where), values)
                if last:
                    nc.sync.dma_start(out_rows[t], pages[t][:])

        def quantize_z(c, z_bf):
            return quantize(f"z{c}", z_bf[:].rearrange("p j t -> p (j t)"), CHUNK)

        w3_bf = keep.tile([P, PACK * N], BF16, name="w3_bf", tag="w2_codes", align_bytes=64)
        round_weight(nc.scalar.copy, w3_bf, w3_raw[0], 0)

        first = keep.tile([P, 2, PACK, CHUNK], F32, name="first")
        ends0 = keep.tile([P, 2, PACK, CHUNK], F32, name="ends0")
        for t in range(PACK):
            nc.vector.tensor_copy(first[:, 0, t, :], y_rows[t][:].indirect(part(l_n1, 0)))
        for t in range(PACK):
            nc.vector.tensor_copy(first[:, 1, t, :], d_rows[t][:].indirect(part(l_n2, 0)))
            nc.vector.tensor_tensor(ends0[:, 0, t, :], d_banks[t][:, cols(0)], first[:, 0, t, :], ALU.min)
            nc.vector.tensor_tensor(ends0[:, 1, t, :], y_banks[t][:, cols(0)], first[:, 1, t, :], ALU.max)
        gap0 = keep.tile([P, PACK, CHUNK], F32, name="gap0")
        nc.vector.tensor_tensor(gap0[:], ends0[:, 1], ends0[:, 0], ALU.subtract)
        z_bf = keep.tile([P, CHUNK, PACK], BF16, name="z_bf0", tag="ring", align_bytes=64)
        nc.vector.tensor_tensor(z_bf[:], gap0[:].rearrange("p t j -> p j t"), gain_wide, ALU.mult)
        w3_q = quantize("w3", w3_bf[:], N)
        got = fetch(1)
        z_q = quantize_z(0, z_bf)
        late_acc = psum.tile([P, 2, CHUNK], F32, name="bank0")
        for c in range(1, CHUNKS):
            if c == 1:
                jobs = layer(0, z_q, [0], 4) + layer(0, z_q, [1, 2, 3], 5)
            elif c == 2:
                jobs = layer(1, z_q, [0, 1, 2, 3], 6)
            else:
                jobs = layer(2, z_q, [0, 1, 2], 7)
                product(late_acc[:, 0, :], w3_q, 3, z_q)
            ends = keep.tile([P, 2, PACK, CHUNK], F32, name=f"ends{c}", tag="ring", align_bytes=64)
            for t in range(PACK):
                nc.vector.tensor_tensor(ends[:, 0, t, :], got[:, 0, t, :], d_rows[t][:, cols(c)], ALU.min)
            for t in range(PACK):
                nc.vector.tensor_tensor(ends[:, 1, t, :], y_rows[t][:, cols(c)], got[:, 1, t, :], ALU.max)
            if c + 1 < CHUNKS:
                got = fetch(c + 1)
            gap = keep.tile([P, PACK, CHUNK], F32, name=f"gap{c}")
            nc.gpsimd.tensor_tensor(gap[:], ends[:, 1], ends[:, 0], ALU.subtract)
            z_bf = keep.tile([P, CHUNK, PACK], BF16, name=f"z_bf{c}", tag="ring", align_bytes=64)
            nc.gpsimd.tensor_tensor(z_bf[:], gap[:].rearrange("p t j -> p j t"), gain_wide, ALU.mult)
            put(jobs, False)
            z_q = quantize_z(c, z_bf)
        jobs = layer(3, z_q, [0], 1) + layer(3, z_q, [1, 2], 2)
        product(late_acc[:, 1, :], w3_q, 3, z_q)
        late = keep.tile([P, 2 * CHUNK], F32, name="late")
        nc.scalar.copy(late[:], late_acc[:].rearrange("p c j -> p (c j)"))
        put(jobs + [(3, l_n3[:, 2 * CHUNK // LIST_ROWS :], late[:])], True)
